import numpy as np
CORES = [50,106,114,52,108,116]
N = 6
TK = 128
NT = N * TK
EPS = 0.01
def setup_inputs(rng):
    x = (rng.standard_normal((N, 128, TK), dtype=np.float32) * (0.5 + np.arange(N, dtype=np.float32).reshape(N, 1, 1) / N) + rng.standard_normal((N, 128, 1), dtype=np.float32))
    return {"x": x, "dy": (rng.standard_normal((N, 128, TK), dtype=np.float32) + 0.5 * x + rng.standard_normal((1, 128, 1), dtype=np.float32))}
def setup_inputs_big(rng):
    d = setup_inputs(rng)
    for k in ("x", "dy"): d[k] = (d[k].astype(np.float32) * 1024.0).astype(d[k].dtype)
    return d
def setup_inputs_small(rng):
    d = setup_inputs(rng)
    for k in ("x", "dy"): d[k] = (d[k].astype(np.float32) * (1 / 1024.0)).astype(d[k].dtype)
    return d
def setup_inputs_apart(rng):
    d = setup_inputs(rng)
    f = (10.0 ** rng.permutation(np.linspace(-1.5, 1.5, N))).astype(np.float32).reshape(N, 1, 1)
    for k in ("x", "dy"): d[k] = (d[k].astype(np.float32) * f).astype(d[k].dtype)
    return d
def setup_inputs_mixed(rng):
    d = setup_inputs(rng)
    f = (10.0 ** rng.uniform(-3, 3, (1, 128, 1))).astype(np.float32); shape = rng.integers(3, size=(1, 128, 1))
    for k in ("x", "dy"):
        x = d[k].astype(np.float32)
        m = x.mean(axis=(0, 2), keepdims=True); level = m + np.sign(x - m) * np.abs(x - m).mean(axis=(0, 2), keepdims=True) * rng.uniform(0.9, 1.1, x.shape).astype(np.float32)
        other = x * np.where(rng.random(x.shape) < 0.5, 0.1, 1.0).astype(np.float32)
        d[k] = (np.where(shape == 1, level, np.where(shape == 2, other, x)) * f).astype(d[k].dtype)
    return d
def setup_inputs_offset(rng):
    d = setup_inputs(rng)
    x = d["x"]; spread = x.std(axis=(0, 2), keepdims=True)
    d["x"] = (x + spread * rng.uniform(16, 48, (1, 128, 1)) * rng.choice([-1.0, 1.0], (1, 128, 1))).astype(np.float32)
    return d
def reference(x, dy):
    X = x.astype(np.float64)
    mu = X.sum(axis=(0, 2)).reshape(1, 128, 1) / NT
    rs = 1.0 / np.sqrt(((X - mu) ** 2).sum(axis=(0, 2)).reshape(1, 128, 1) / NT + EPS)
    n = (X - mu) * rs
    DY = dy.astype(np.float64)
    a = DY.sum(axis=(0, 2)).reshape(1, 128, 1) / NT; c = (DY * n).sum(axis=(0, 2)).reshape(1, 128, 1) / NT
    return {"dx": (rs * (DY - a - n * c)).astype(np.float32)}

@@ -1,0 +1,212 @@
+from concourse.bass import DstId, RemoteDMATransfer
+from concourse.mybir import AluOpType, AxisListType, ActivationFunctionType
+
+N = 6
+TK = 128
+NT = N * TK
+EPS = 0.01
+NS = 4
+NEAR_ENGINES = 4
+
+SCRATCH = {
+    "xs": ("sbuf", [128, TK], "float32"),
+    "dys": ("sbuf", [128, TK], "float32"),
+    "land": ("sbuf", [128, N * NS], "float32"),
+    "col": ("sbuf", [128, 32], "float32"),
+    "j1": ("sbuf", [128, TK], "float32"),
+    "j2": ("sbuf", [128, TK], "float32"),
+    "prod": ("sbuf", [128, TK], "float32"),
+    "j6a": ("sbuf", [128, 8], "float32"),
+    "j6b": ("sbuf", [128, 8], "float32"),
+    "nd6": ("sbuf", [128, 8], "float32"),
+    "e6": ("sbuf", [128, 8], "float32"),
+    "br": ("sbuf", [128, TK], "float32"),
+    "out": ("sbuf", [128, TK], "float32"),
+    "xc": ("psum", [128, 512], "float32"),
+    "t2": ("psum", [128, 512], "float32"),
+}
+SEMAPHORES = ["ldx", "ldy", "st", "near", "far", "sent"] + ["k%d" % i for i in range(32)]
+
+
+def _low(mask, n):
+    out, b = 0, 1
+    while n > 0:
+        if mask & b:
+            out |= b
+            n -= 1
+        b <<= 1
+    return out
+
+
+def _count(mask):
+    return bin(mask).count("1")
+
+
+def _plan(T, topo):
+    cores = list(T.cores)
+    chips = []
+    for c in cores:
+        if topo.chip(c) not in chips:
+            chips.append(topo.chip(c))
+    order = [c for ch in chips for c in cores if topo.chip(c) == ch]
+    slot = {c: i for i, c in enumerate(order)}
+    home = {c: [d for d in order if topo.chip(d) == topo.chip(c)] for c in cores}
+    away = {c: [d for d in order if topo.chip(d) != topo.chip(c)] for c in cores}
+    sender = {}
+    for c in order:
+        ch = topo.chip(c)
+        if ch not in sender and all(topo.may_write(c, d) for d in away[c]):
+            sender[ch] = c
+    mask = {}
+    for c in cores:
+        mates = [d for d in home[c] if d != c]
+        if sender[topo.chip(c)] == c:
+            m = -1
+            for d in mates + away[c]:
+                m &= topo.mask(c, d)
+            mask[c] = m
+        else:
+            m = -1
+            for d in mates:
+                m &= topo.mask(c, d)
+            mask[c] = _low(m, NEAR_ENGINES)
+    return slot, home, away, sender, mask
+
+
+def rank_program(g, core, T, topo):
+    if T.rank_of(core) is None:
+        return
+    slot, home, away, sender, mask = _plan(T, topo)
+    v, s, sy = g.vector, g.scalar, g.sync
+    sem = T.sem
+    A, X, F = AluOpType, AxisListType.X, ActivationFunctionType
+    nk = [0]
+
+    def new():
+        nk[0] += 1
+        return sem["k%d" % (nk[0] - 1)]
+
+    ncol = [0]
+
+    def column():
+        ncol[0] += 1
+        return T.col[:, ncol[0] - 1:ncol[0]]
+
+    o = slot[core] * NS
+    negm, sdy, m2, cc = (T.land[:, o + i:o + i + 1] for i in range(NS))
+    xc = T.xc[:, 0:TK]
+    t2 = T.t2[:, 0:TK]
+
+    sy.dma_start(T.xs[:], T.x[:]).then_inc(sem.ldx, 16)
+    s.dma_start(T.dys[:], T.dy[:]).then_inc(sem.ldy, 16)
+
+    a1, a2, a3, a4, a5, b1, b2 = (new() for _ in range(7))
+    nsx = column()
+    v.wait_ge(sem.ldx, 16)
+    v.tensor_reduce(nsx, T.xs[:], X, A.add, negate=True).then_inc(a1, 1)
+    v.wait_ge(a1, 1)
+    v.tensor_scalar(negm, nsx, 1.0 / TK, None, A.mult).then_inc(a2, 1)
+    v.wait_ge(a2, 1)
+    v.tensor_scalar(xc, T.xs[:], negm, None, A.add).then_inc(a3, 1)
+    v.wait_ge(a3, 1)
+    v.wait_ge(sem.ldy, 16)
+    v.tensor_tensor(T.prod[:], T.dys[:], xc, A.mult).then_inc(a4, 1)
+    v.wait_ge(a4, 1)
+    v.tensor_reduce(cc, T.prod[:], X, A.add).then_inc(a5, 1)
+
+    s.wait_ge(sem.ldy, 16)
+    s.activation(T.j1[:], T.dys[:], F.Copy, accum_out=sdy).then_inc(b1, 1)
+    s.wait_ge(sem.ldx, 16)
+    s.wait_ge(a2, 1)
+    s.activation(T.j2[:], T.xs[:], F.Square, bias=negm, accum_out=m2).then_inc(b2, 1)
+
+    g.wait_ge(a2, 1)
+    g.wait_ge(b1, 1)
+    g.wait_ge(b2, 1)
+    g.wait_ge(a5, 1)
+    mine = T.land[:, o:o + NS]
+    mates = [d for d in home[core] if d != core]
+    sent = 0
+    g.remote_dma_fused(
+        [RemoteDMATransfer(dst_ids=[DstId(rid=topo.addr(d)[0], pnc=topo.addr(d)[1]) for d in mates],
+                           dma_engine_mask=mask[core], remote_sem=sem.near,
+                           srcs=[mine], dsts=[mine for _ in mates], alu_op=0)],
+        local_sem=sem.sent)
+    sent += _count(mask[core])
+    near = sum(_count(mask[d]) for d in mates)
+    if sender[topo.chip(core)] == core:
+        lo = min(slot[d] for d in home[core]) * NS
+        block = T.land[:, lo:lo + NS * len(home[core])]
+        g.wait_ge(sem.near, near)
+        g.remote_dma_fused(
+            [RemoteDMATransfer(dst_ids=[DstId(rid=topo.addr(d)[0], pnc=topo.addr(d)[1]) for d in away[core]],
+                               dma_engine_mask=mask[core], remote_sem=sem.far,
+                               srcs=[block], dsts=[block for _ in away[core]], alu_op=0)],
+            local_sem=sem.sent)
+        sent += _count(mask[core])
+    g.wait_ge(sem.sent, sent)
+    far = sum(_count(mask[c]) for ch, c in sender.items() if ch != topo.chip(core))
+
+    w = N * NS
+    NM, SD, MM, CC = (T.land[:, i:w:NS] for i in range(NS))
+    c1, c2, c3, c4, c5, c6, c7, c8, c9, c10, c11, c12, c13, c14, c15, c16 = (new() for _ in range(16))
+    d1, d2, d3 = (new() for _ in range(3))
+    mu6, bcol, acc, sd, se, sc_, nssd, ncov, vv, rs2, nb, na, dn, wc = (column() for _ in range(14))
+    kk = float(TK) / (36.0 * NT)
+
+    s.wait_ge(sem.near, near)
+    s.wait_ge(sem.far, far)
+    s.wait_ge(b1, 1)
+    s.wait_ge(b2, 1)
+    s.activation(T.j6a[:, 0:N], MM, F.Identity, bias=EPS / N, scale=1.0 / NT, accum_out=bcol).then_inc(d1, 1)
+    s.wait_ge(c1, 1)
+    s.activation(T.j6b[:, 0:N], NM, F.Square, bias=mu6, scale=float(N), accum_out=acc).then_inc(d2, 1)
+    s.wait_ge(d1, 1)
+    s.wait_ge(d2, 1)
+    s.activation(sd, acc, F.Sqrt, bias=bcol, scale=kk).then_inc(d3, 1)
+
+    nd6 = T.nd6[:, 0:N]
+    e6 = T.e6[:, 0:N]
+    v.wait_ge(sem.near, near)
+    v.wait_ge(sem.far, far)
+    v.wait_ge(b1, 1)
+    v.wait_ge(b2, 1)
+    v.wait_ge(a5, 1)
+    v.tensor_reduce(mu6, NM, X, A.add, negate=True).then_inc(c1, 1)
+    v.wait_ge(c1, 1)
+    v.tensor_scalar(nd6, NM, float(N), mu6, A.mult, A.add).then_inc(c2, 1)
+    v.tensor_reduce(sc_, CC, X, A.add).then_inc(c5, 1)
+    v.tensor_reduce(nssd, SD, X, A.add, negate=True).then_inc(c6, 1)
+    v.wait_ge(c2, 1)
+    v.tensor_tensor(e6, nd6, SD, A.mult).then_inc(c3, 1)
+    v.tensor_scalar(dn, T.nd6[:, slot[core]:slot[core] + 1], -1.0 / N, None, A.mult).then_inc(c12, 1)
+    v.wait_ge(c6, 1)
+    v.tensor_scalar(na, nssd, 1.0 / NT, None, A.mult).then_inc(c11, 1)
+    v.wait_ge(c3, 1)
+    v.tensor_reduce(se, e6, X, A.add).then_inc(c4, 1)
+    v.wait_ge(d1, 1)
+    v.wait_ge(d2, 1)
+    v.tensor_scalar(vv, acc, kk, bcol, A.mult, A.add).then_inc(c8, 1)
+    v.wait_ge(c4, 1)
+    v.wait_ge(c5, 1)
+    v.tensor_scalar(ncov, se, 1.0 / N, sc_, A.mult, A.subtract).then_inc(c7, 1)
+    v.wait_ge(c8, 1)
+    v.reciprocal(rs2, vv).then_inc(c9, 1)
+    v.wait_ge(c7, 1)
+    v.wait_ge(c9, 1)
+    v.tensor_scalar(nb, ncov, 1.0 / NT, rs2, A.mult, A.mult).then_inc(c10, 1)
+    v.wait_ge(c10, 1)
+    v.wait_ge(c11, 1)
+    v.wait_ge(c12, 1)
+    v.tensor_scalar(wc, dn, nb, na, A.mult, A.add).then_inc(c13, 1)
+    v.wait_ge(c13, 1)
+    v.tensor_scalar(t2, xc, nb, wc, A.mult, A.add).then_inc(c14, 1)
+    v.wait_ge(c14, 1)
+    v.tensor_tensor(T.br[:], T.dys[:], t2, A.add).then_inc(c15, 1)
+    v.wait_ge(c15, 1)
+    v.wait_ge(d3, 1)
+    v.tensor_scalar(T.out[:], T.br[:], rs2, sd, A.mult, A.mult).then_inc(c16, 1)
+
+    sy.wait_ge(c16, 1)
+    sy.dma_start(T.dx[:], T.out[:]).then_inc(sem.st, 16)
+    sy.wait_ge(sem.st, 16)

@@ -1,3 +1,4 @@
+import math
 from concourse.bass import DstId, RemoteDMATransfer
 from concourse.mybir import AluOpType, AxisListType, ActivationFunctionType
 
@@ -5,7 +6,7 @@ N = 6
 TK = 128
 NT = N * TK
 EPS = 0.01
-NS = 4
+NS = 8
 NEAR_ENGINES = 4
 
 SCRATCH = {
@@ -13,19 +14,19 @@ SCRATCH = {
     "dys": ("sbuf", [128, TK], "float32"),
     "land": ("sbuf", [128, N * NS], "float32"),
     "col": ("sbuf", [128, 32], "float32"),
-    "j1": ("sbuf", [128, TK], "float32"),
     "j2": ("sbuf", [128, TK], "float32"),
     "prod": ("sbuf", [128, TK], "float32"),
     "j6a": ("sbuf", [128, 8], "float32"),
     "j6b": ("sbuf", [128, 8], "float32"),
-    "nd6": ("sbuf", [128, 8], "float32"),
-    "e6": ("sbuf", [128, 8], "float32"),
+    "ndk": ("sbuf", [128, 8], "float32"),
+    "t12": ("sbuf", [128, 2 * N], "float32"),
+    "ya": ("sbuf", [128, TK], "float32"),
     "br": ("sbuf", [128, TK], "float32"),
     "out": ("sbuf", [128, TK], "float32"),
     "xc": ("psum", [128, 512], "float32"),
     "t2": ("psum", [128, 512], "float32"),
 }
-SEMAPHORES = ["ldx", "ldy", "st", "near", "far", "sent"] + ["k%d" % i for i in range(32)]
+SEMAPHORES = ["ldx", "ldy", "st", "near", "far", "sent", "vs"] + ["k%d" % i for i in range(32)]
 
 
 def _low(mask, n):
@@ -93,37 +94,37 @@ def rank_program(g, core, T, topo):
         return T.col[:, ncol[0] - 1:ncol[0]]
 
     o = slot[core] * NS
-    negm, sdy, m2, cc = (T.land[:, o + i:o + i + 1] for i in range(NS))
+    o_m, o_k, o_s1, o_s2, o_sd, o_ck, o_p0, o_pe = (T.land[:, o + i:o + i + 1] for i in range(NS))
     xc = T.xc[:, 0:TK]
     t2 = T.t2[:, 0:TK]
+    first = T.xs[:, 0:1]
 
     sy.dma_start(T.xs[:], T.x[:]).then_inc(sem.ldx, 16)
     s.dma_start(T.dys[:], T.dy[:]).then_inc(sem.ldy, 16)
 
-    a1, a2, a3, a4, a5, b1, b2 = (new() for _ in range(7))
-    nsx = column()
+    a1, a2, a3, b2 = (new() for _ in range(4))
+    v.memset(o_p0, 0.0).then_inc(sem.vs, 1)
+    v.memset(o_pe, TK * EPS).then_inc(sem.vs, 1)
     v.wait_ge(sem.ldx, 16)
-    v.tensor_reduce(nsx, T.xs[:], X, A.add, negate=True).then_inc(a1, 1)
-    v.wait_ge(a1, 1)
-    v.tensor_scalar(negm, nsx, 1.0 / TK, None, A.mult).then_inc(a2, 1)
-    v.wait_ge(a2, 1)
-    v.tensor_scalar(xc, T.xs[:], negm, None, A.add).then_inc(a3, 1)
-    v.wait_ge(a3, 1)
+    v.tensor_scalar(xc, T.xs[:], first, None, A.subtract).then_inc(a1, 1)
+    v.tensor_copy(o_k, first).then_inc(sem.vs, 1)
     v.wait_ge(sem.ldy, 16)
-    v.tensor_tensor(T.prod[:], T.dys[:], xc, A.mult).then_inc(a4, 1)
-    v.wait_ge(a4, 1)
-    v.tensor_reduce(cc, T.prod[:], X, A.add).then_inc(a5, 1)
+    v.wait_ge(a1, 1)
+    v.tensor_tensor(T.prod[:], T.dys[:], xc, A.mult).then_inc(a3, 1)
+    v.tensor_reduce(o_s1, xc, X, A.add).then_inc(a2, 1)
+    v.tensor_reduce(o_sd, T.dys[:], X, A.add).then_inc(sem.vs, 1)
+    v.wait_ge(a3, 1)
+    v.tensor_reduce(o_ck, T.prod[:], X, A.add).then_inc(sem.vs, 1)
+    v.wait_ge(a2, 1)
+    v.tensor_scalar(o_m, first, float(TK), o_s1, A.mult, A.add).then_inc(sem.vs, 1)
+    nvs = 6
 
-    s.wait_ge(sem.ldy, 16)
-    s.activation(T.j1[:], T.dys[:], F.Copy, accum_out=sdy).then_inc(b1, 1)
     s.wait_ge(sem.ldx, 16)
-    s.wait_ge(a2, 1)
-    s.activation(T.j2[:], T.xs[:], F.Square, bias=negm, accum_out=m2).then_inc(b2, 1)
+    s.activation(T.j2[:], T.xs[:], F.Square, bias=first, scale=-1.0, accum_out=o_s2).then_inc(b2, 1)
 
-    g.wait_ge(a2, 1)
-    g.wait_ge(b1, 1)
     g.wait_ge(b2, 1)
-    g.wait_ge(a5, 1)
+    g.wait_ge(a2, 1)
+    g.wait_ge(sem.vs, nvs)
     mine = T.land[:, o:o + NS]
     mates = [d for d in home[core] if d != core]
     sent = 0
@@ -148,64 +149,67 @@ def rank_program(g, core, T, topo):
     far = sum(_count(mask[c]) for ch, c in sender.items() if ch != topo.chip(core))
 
     w = N * NS
-    NM, SD, MM, CC = (T.land[:, i:w:NS] for i in range(NS))
-    c1, c2, c3, c4, c5, c6, c7, c8, c9, c10, c11, c12, c13, c14, c15, c16 = (new() for _ in range(16))
+    MS, KK, S1, _s2, SD, CK = (T.land[:, i:w:NS] for i in range(6))
+    S2E = T.land[:, 3:w:4]
+    c1, c2, c3, c4, c8, c9, c10, c14, c15, c16 = (new() for _ in range(10))
+    f1, f2, f3, f4, f5, f6, f7 = (new() for _ in range(7))
     d1, d2, d3 = (new() for _ in range(3))
-    mu6, bcol, acc, sd, se, sc_, nssd, ncov, vv, rs2, nb, na, dn, wc = (column() for _ in range(14))
-    kk = float(TK) / (36.0 * NT)
+    smn, ss2, nssd, bcol, na, gown, vv, rp, s768, nb, db, acc, sd = (column() for _ in range(13))
+    kq = float(TK) / float(NT * NT)
+    r768 = math.sqrt(float(NT))
 
     s.wait_ge(sem.near, near)
     s.wait_ge(sem.far, far)
-    s.wait_ge(b1, 1)
-    s.wait_ge(b2, 1)
-    s.activation(T.j6a[:, 0:N], MM, F.Identity, bias=EPS / N, scale=1.0 / NT, accum_out=bcol).then_inc(d1, 1)
+    s.wait_ge(a2, 1)
+    s.wait_ge(sem.vs, nvs)
+    s.activation(T.j6a[:, 0:N], S1, F.Square, scale=math.sqrt(1.0 / TK), accum_out=db).then_inc(d1, 1)
     s.wait_ge(c1, 1)
-    s.activation(T.j6b[:, 0:N], NM, F.Square, bias=mu6, scale=float(N), accum_out=acc).then_inc(d2, 1)
-    s.wait_ge(d1, 1)
+    s.activation(T.j6b[:, 0:N], MS, F.Square, bias=smn, scale=float(N), accum_out=acc).then_inc(d2, 1)
     s.wait_ge(d2, 1)
-    s.activation(sd, acc, F.Sqrt, bias=bcol, scale=kk).then_inc(d3, 1)
+    s.wait_ge(f4, 1)
+    s.activation(sd, acc, F.Sqrt, bias=bcol, scale=kq).then_inc(d3, 1)
 
-    nd6 = T.nd6[:, 0:N]
-    e6 = T.e6[:, 0:N]
+    ndk = T.ndk[:, 0:N]
     v.wait_ge(sem.near, near)
     v.wait_ge(sem.far, far)
-    v.wait_ge(b1, 1)
     v.wait_ge(b2, 1)
-    v.wait_ge(a5, 1)
-    v.tensor_reduce(mu6, NM, X, A.add, negate=True).then_inc(c1, 1)
-    v.wait_ge(c1, 1)
-    v.tensor_scalar(nd6, NM, float(N), mu6, A.mult, A.add).then_inc(c2, 1)
-    v.tensor_reduce(sc_, CC, X, A.add).then_inc(c5, 1)
-    v.tensor_reduce(nssd, SD, X, A.add, negate=True).then_inc(c6, 1)
-    v.wait_ge(c2, 1)
-    v.tensor_tensor(e6, nd6, SD, A.mult).then_inc(c3, 1)
-    v.tensor_scalar(dn, T.nd6[:, slot[core]:slot[core] + 1], -1.0 / N, None, A.mult).then_inc(c12, 1)
-    v.wait_ge(c6, 1)
-    v.tensor_scalar(na, nssd, 1.0 / NT, None, A.mult).then_inc(c11, 1)
-    v.wait_ge(c3, 1)
-    v.tensor_reduce(se, e6, X, A.add).then_inc(c4, 1)
+    v.wait_ge(sem.vs, nvs)
+    v.tensor_reduce(smn, MS, X, A.add, negate=True).then_inc(c1, 1)
+    v.tensor_reduce(ss2, S2E, X, A.add).then_inc(f1, 1)
+    v.tensor_reduce(nssd, SD, X, A.add, negate=True).then_inc(f2, 1)
+    v.tensor_scalar(T.t12[:, N:2 * N], CK, float(NT), None, A.mult).then_inc(f3, 1)
     v.wait_ge(d1, 1)
+    v.wait_ge(f1, 1)
+    v.tensor_scalar(bcol, db, -1.0, ss2, A.mult, A.add).then_inc(f4, 1)
+    v.wait_ge(c1, 1)
+    v.tensor_scalar(ndk, KK, float(NT), smn, A.mult, A.add).then_inc(c2, 1)
+    v.wait_ge(f2, 1)
+    v.tensor_scalar(na, nssd, 1.0 / NT, None, A.mult).then_inc(f5, 1)
+    v.wait_ge(c2, 1)
+    v.tensor_tensor(T.t12[:, 0:N], ndk, SD, A.mult).then_inc(c3, 1)
+    v.tensor_scalar(gown, T.ndk[:, slot[core]:slot[core] + 1], 1.0 / NT, None, A.mult).then_inc(f6, 1)
     v.wait_ge(d2, 1)
-    v.tensor_scalar(vv, acc, kk, bcol, A.mult, A.add).then_inc(c8, 1)
-    v.wait_ge(c4, 1)
-    v.wait_ge(c5, 1)
-    v.tensor_scalar(ncov, se, 1.0 / N, sc_, A.mult, A.subtract).then_inc(c7, 1)
+    v.wait_ge(f4, 1)
+    v.tensor_scalar(vv, acc, kq, bcol, A.mult, A.add).then_inc(c8, 1)
+    v.wait_ge(f5, 1)
+    v.tensor_scalar(T.ya[:], T.dys[:], na, r768, A.add, A.mult).then_inc(f7, 1)
+    v.wait_ge(c3, 1)
+    v.wait_ge(f3, 1)
+    v.tensor_reduce(s768, T.t12[:], X, A.add).then_inc(c4, 1)
     v.wait_ge(c8, 1)
-    v.reciprocal(rs2, vv).then_inc(c9, 1)
-    v.wait_ge(c7, 1)
+    v.reciprocal(rp, vv).then_inc(c9, 1)
+    v.wait_ge(c4, 1)
     v.wait_ge(c9, 1)
-    v.tensor_scalar(nb, ncov, 1.0 / NT, rs2, A.mult, A.mult).then_inc(c10, 1)
+    v.tensor_scalar(nb, s768, rp, -1.0 / r768, A.mult, A.mult).then_inc(c10, 1)
     v.wait_ge(c10, 1)
-    v.wait_ge(c11, 1)
-    v.wait_ge(c12, 1)
-    v.tensor_scalar(wc, dn, nb, na, A.mult, A.add).then_inc(c13, 1)
-    v.wait_ge(c13, 1)
-    v.tensor_scalar(t2, xc, nb, wc, A.mult, A.add).then_inc(c14, 1)
+    v.wait_ge(f6, 1)
+    v.tensor_scalar(t2, xc, gown, nb, A.add, A.mult).then_inc(c14, 1)
     v.wait_ge(c14, 1)
-    v.tensor_tensor(T.br[:], T.dys[:], t2, A.add).then_inc(c15, 1)
+    v.wait_ge(f7, 1)
+    v.tensor_tensor(T.br[:], T.ya[:], t2, A.add).then_inc(c15, 1)
     v.wait_ge(c15, 1)
     v.wait_ge(d3, 1)
-    v.tensor_scalar(T.out[:], T.br[:], rs2, sd, A.mult, A.mult).then_inc(c16, 1)
+    v.tensor_scalar(T.out[:], T.br[:], rp, sd, A.mult, A.mult).then_inc(c16, 1)
 
     sy.wait_ge(c16, 1)
     sy.dma_start(T.dx[:], T.out[:]).then_inc(sem.st, 16)

@@ -93,21 +93,32 @@ def rank_program(g, core, T, topo):
         ncol[0] += 1
         return T.col[:, ncol[0] - 1:ncol[0]]
 
+    def write(dests, src, dst, remote_sem):
+        g.remote_dma_fused(
+            [RemoteDMATransfer(dst_ids=[DstId(rid=topo.addr(d)[0], pnc=topo.addr(d)[1]) for d in dests],
+                               dma_engine_mask=mask[core], remote_sem=remote_sem,
+                               srcs=[src], dsts=[dst for _ in dests], alu_op=0)],
+            local_sem=sem.sent)
+        return _count(mask[core])
+
     o = slot[core] * NS
-    o_m, o_k, o_s1, o_s2, o_sd, o_ck, o_p0, o_pe = (T.land[:, o + i:o + i + 1] for i in range(NS))
+    o_m, o_s1, o_s2, o_sd, o_ck, o_p0, o_pe, o_k = (T.land[:, o + i:o + i + 1] for i in range(NS))
     xc = T.xc[:, 0:TK]
     t2 = T.t2[:, 0:TK]
     first = T.xs[:, 0:1]
+    mates = [d for d in home[core] if d != core]
 
     sy.dma_start(T.xs[:], T.x[:]).then_inc(sem.ldx, 16)
     s.dma_start(T.dys[:], T.dy[:]).then_inc(sem.ldy, 16)
 
-    a1, a2, a3, b2 = (new() for _ in range(4))
+    g.wait_ge(sem.ldx, 16)
+    sent = write(mates, first, o_k, sem.near)
+
+    a1, a2, a3, b1, b2 = (new() for _ in range(5))
     v.memset(o_p0, 0.0).then_inc(sem.vs, 1)
     v.memset(o_pe, TK * EPS).then_inc(sem.vs, 1)
     v.wait_ge(sem.ldx, 16)
     v.tensor_scalar(xc, T.xs[:], first, None, A.subtract).then_inc(a1, 1)
-    v.tensor_copy(o_k, first).then_inc(sem.vs, 1)
     v.wait_ge(sem.ldy, 16)
     v.wait_ge(a1, 1)
     v.tensor_tensor(T.prod[:], T.dys[:], xc, A.mult).then_inc(a3, 1)
@@ -117,40 +128,30 @@ def rank_program(g, core, T, topo):
     v.tensor_reduce(o_ck, T.prod[:], X, A.add).then_inc(sem.vs, 1)
     v.wait_ge(a2, 1)
     v.tensor_scalar(o_m, first, float(TK), o_s1, A.mult, A.add).then_inc(sem.vs, 1)
-    nvs = 6
+    nvs = 5
 
     s.wait_ge(sem.ldx, 16)
     s.activation(T.j2[:], T.xs[:], F.Square, bias=first, scale=-1.0, accum_out=o_s2).then_inc(b2, 1)
+    s.activation(o_k, first, F.Copy).then_inc(b1, 1)
 
     g.wait_ge(b2, 1)
     g.wait_ge(a2, 1)
     g.wait_ge(sem.vs, nvs)
-    mine = T.land[:, o:o + NS]
-    mates = [d for d in home[core] if d != core]
-    sent = 0
-    g.remote_dma_fused(
-        [RemoteDMATransfer(dst_ids=[DstId(rid=topo.addr(d)[0], pnc=topo.addr(d)[1]) for d in mates],
-                           dma_engine_mask=mask[core], remote_sem=sem.near,
-                           srcs=[mine], dsts=[mine for _ in mates], alu_op=0)],
-        local_sem=sem.sent)
-    sent += _count(mask[core])
-    near = sum(_count(mask[d]) for d in mates)
+    rest = T.land[:, o:o + NS - 1]
+    sent += write(mates, rest, rest, sem.near)
+    near = sum(2 * _count(mask[d]) for d in mates)
     if sender[topo.chip(core)] == core:
         lo = min(slot[d] for d in home[core]) * NS
         block = T.land[:, lo:lo + NS * len(home[core])]
+        g.wait_ge(b1, 1)
         g.wait_ge(sem.near, near)
-        g.remote_dma_fused(
-            [RemoteDMATransfer(dst_ids=[DstId(rid=topo.addr(d)[0], pnc=topo.addr(d)[1]) for d in away[core]],
-                               dma_engine_mask=mask[core], remote_sem=sem.far,
-                               srcs=[block], dsts=[block for _ in away[core]], alu_op=0)],
-            local_sem=sem.sent)
-        sent += _count(mask[core])
+        sent += write(away[core], block, block, sem.far)
     g.wait_ge(sem.sent, sent)
     far = sum(_count(mask[c]) for ch, c in sender.items() if ch != topo.chip(core))
 
     w = N * NS
-    MS, KK, S1, _s2, SD, CK = (T.land[:, i:w:NS] for i in range(6))
-    S2E = T.land[:, 3:w:4]
+    MS, S1, SD, CK, KK = (T.land[:, i:w:NS] for i in (0, 1, 3, 4, 7))
+    S2E = T.land[:, 2:w:4]
     c1, c2, c3, c4, c8, c9, c10, c14, c15, c16 = (new() for _ in range(10))
     f1, f2, f3, f4, f5, f6, f7 = (new() for _ in range(7))
     d1, d2, d3 = (new() for _ in range(3))
@@ -172,6 +173,7 @@ def rank_program(g, core, T, topo):
     ndk = T.ndk[:, 0:N]
     v.wait_ge(sem.near, near)
     v.wait_ge(sem.far, far)
+    v.wait_ge(b1, 1)
     v.wait_ge(b2, 1)
     v.wait_ge(sem.vs, nvs)
     v.tensor_reduce(smn, MS, X, A.add, negate=True).then_inc(c1, 1)

@@ -7,7 +7,7 @@ TK = 128
 NT = N * TK
 EPS = 0.01
 NS = 8
-NEAR_ENGINES = 4
+ENGINES = 8
 
 SCRATCH = {
     "xs": ("sbuf", [128, TK], "float32"),
@@ -15,18 +15,22 @@ SCRATCH = {
     "land": ("sbuf", [128, N * NS], "float32"),
     "col": ("sbuf", [128, 32], "float32"),
     "j2": ("sbuf", [128, TK], "float32"),
+    "j3": ("sbuf", [128, TK], "float32"),
+    "j4": ("sbuf", [128, TK], "float32"),
     "prod": ("sbuf", [128, TK], "float32"),
     "j6a": ("sbuf", [128, 8], "float32"),
     "j6b": ("sbuf", [128, 8], "float32"),
+    "j6c": ("sbuf", [128, 8], "float32"),
     "ndk": ("sbuf", [128, 8], "float32"),
     "t12": ("sbuf", [128, 2 * N], "float32"),
     "ya": ("sbuf", [128, TK], "float32"),
-    "br": ("sbuf", [128, TK], "float32"),
+    "yb": ("sbuf", [128, TK], "float32"),
     "out": ("sbuf", [128, TK], "float32"),
     "xc": ("psum", [128, 512], "float32"),
+    "xg": ("psum", [128, 512], "float32"),
     "t2": ("psum", [128, 512], "float32"),
 }
-SEMAPHORES = ["ldx", "ldy", "st", "near", "far", "sent", "vs"] + ["k%d" % i for i in range(32)]
+SEMAPHORES = ["ldx", "ldy", "st", "near", "far", "sent", "vs", "ss"] + ["k%d" % i for i in range(48)]
 
 
 def _low(mask, n):
@@ -53,31 +57,26 @@ def _plan(T, topo):
     slot = {c: i for i, c in enumerate(order)}
     home = {c: [d for d in order if topo.chip(d) == topo.chip(c)] for c in cores}
     away = {c: [d for d in order if topo.chip(d) != topo.chip(c)] for c in cores}
-    sender = {}
-    for c in order:
-        ch = topo.chip(c)
-        if ch not in sender and all(topo.may_write(c, d) for d in away[c]):
-            sender[ch] = c
+    far = {c: [] for c in cores}
+    for ch in chips:
+        ranks = [c for c in order if topo.chip(c) == ch]
+        can = {d: [c for c in ranks if topo.may_write(c, d)] for d in away[ranks[0]]}
+        for d in sorted(can, key=lambda e: len(can[e])):
+            c = min(can[d], key=lambda e: (len(far[e]), topo.die(e) != topo.die(d)))
+            far[c].append(d)
     mask = {}
     for c in cores:
-        mates = [d for d in home[c] if d != c]
-        if sender[topo.chip(c)] == c:
-            m = -1
-            for d in mates + away[c]:
-                m &= topo.mask(c, d)
-            mask[c] = m
-        else:
-            m = -1
-            for d in mates:
-                m &= topo.mask(c, d)
-            mask[c] = _low(m, NEAR_ENGINES)
-    return slot, home, away, sender, mask
+        m = -1
+        for d in [e for e in home[c] if e != c] + far[c]:
+            m &= topo.mask(c, d)
+        mask[c] = _low(m, min(ENGINES, _count(m)))
+    return slot, home, far, mask
 
 
 def rank_program(g, core, T, topo):
     if T.rank_of(core) is None:
         return
-    slot, home, away, sender, mask = _plan(T, topo)
+    slot, home, far_of, mask = _plan(T, topo)
     v, s, sy = g.vector, g.scalar, g.sync
     sem = T.sem
     A, X, F = AluOpType, AxisListType.X, ActivationFunctionType
@@ -104,6 +103,7 @@ def rank_program(g, core, T, topo):
     o = slot[core] * NS
     o_m, o_s1, o_s2, o_sd, o_ck, o_p0, o_pe, o_k = (T.land[:, o + i:o + i + 1] for i in range(NS))
     xc = T.xc[:, 0:TK]
+    xg = T.xg[:, 0:TK]
     t2 = T.t2[:, 0:TK]
     first = T.xs[:, 0:1]
     mates = [d for d in home[core] if d != core]
@@ -114,7 +114,7 @@ def rank_program(g, core, T, topo):
     g.wait_ge(sem.ldx, 16)
     sent = write(mates, first, o_k, sem.near)
 
-    a1, a2, a3, b1, b2 = (new() for _ in range(5))
+    a1, a3, b1 = (new() for _ in range(3))
     v.memset(o_p0, 0.0).then_inc(sem.vs, 1)
     v.memset(o_pe, TK * EPS).then_inc(sem.vs, 1)
     v.wait_ge(sem.ldx, 16)
@@ -122,96 +122,120 @@ def rank_program(g, core, T, topo):
     v.wait_ge(sem.ldy, 16)
     v.wait_ge(a1, 1)
     v.tensor_tensor(T.prod[:], T.dys[:], xc, A.mult).then_inc(a3, 1)
-    v.tensor_reduce(o_s1, xc, X, A.add).then_inc(a2, 1)
-    v.tensor_reduce(o_sd, T.dys[:], X, A.add).then_inc(sem.vs, 1)
+    v.tensor_reduce(o_s1, xc, X, A.add).then_inc(sem.vs, 1)
     v.wait_ge(a3, 1)
     v.tensor_reduce(o_ck, T.prod[:], X, A.add).then_inc(sem.vs, 1)
-    v.wait_ge(a2, 1)
-    v.tensor_scalar(o_m, first, float(TK), o_s1, A.mult, A.add).then_inc(sem.vs, 1)
-    nvs = 5
+    nvs = 4
 
     s.wait_ge(sem.ldx, 16)
-    s.activation(T.j2[:], T.xs[:], F.Square, bias=first, scale=-1.0, accum_out=o_s2).then_inc(b2, 1)
+    s.activation(T.j2[:], T.xs[:], F.Square, bias=first, scale=-1.0, accum_out=o_s2).then_inc(sem.ss, 1)
+    s.activation(T.j3[:], T.xs[:], F.Copy, accum_out=o_m).then_inc(sem.ss, 1)
+    s.wait_ge(sem.ldy, 16)
+    s.activation(T.j4[:], T.dys[:], F.Copy, accum_out=o_sd).then_inc(sem.ss, 1)
     s.activation(o_k, first, F.Copy).then_inc(b1, 1)
+    nss = 3
 
-    g.wait_ge(b2, 1)
-    g.wait_ge(a2, 1)
+    g.wait_ge(sem.ss, nss)
     g.wait_ge(sem.vs, nvs)
     rest = T.land[:, o:o + NS - 1]
     sent += write(mates, rest, rest, sem.near)
     near = sum(2 * _count(mask[d]) for d in mates)
-    if sender[topo.chip(core)] == core:
+    if far_of[core]:
         lo = min(slot[d] for d in home[core]) * NS
         block = T.land[:, lo:lo + NS * len(home[core])]
         g.wait_ge(b1, 1)
         g.wait_ge(sem.near, near)
-        sent += write(away[core], block, block, sem.far)
+        sent += write(far_of[core], block, block, sem.far)
     g.wait_ge(sem.sent, sent)
-    far = sum(_count(mask[c]) for ch, c in sender.items() if ch != topo.chip(core))
+    far = sum(_count(mask[c]) for c in far_of if core in far_of[c])
+
+    kq = float(TK) / float(NT * NT)
+    r768 = math.sqrt(float(NT))
+
+    e1, e2, e3, e4, e5, e6, e7, e8 = (new() for _ in range(8))
+    q1, own, tc, tt, inv, kqi, u768, cn = (column() for _ in range(8))
+    v.wait_ge(sem.vs, nvs)
+    v.wait_ge(sem.ss, nss)
+    v.tensor_scalar(q1, o_s1, o_s1, -1.0 / TK, A.mult, A.mult).then_inc(e1, 1)
+    v.wait_ge(e1, 1)
+    v.tensor_scalar(own, q1, o_s2, TK * EPS, A.add, A.add).then_inc(e2, 1)
+    s.wait_ge(e2, 1)
+    s.activation(tc, own, F.Sqrt).then_inc(e3, 1)
+    v.wait_ge(e3, 1)
+    v.tensor_scalar(tt, tc, tc, None, A.mult).then_inc(e4, 1)
+    v.wait_ge(e4, 1)
+    v.reciprocal(inv, tt).then_inc(e5, 1)
+    v.wait_ge(e5, 1)
+    v.tensor_scalar(kqi, inv, kq, None, A.mult).then_inc(e6, 1)
+    v.tensor_scalar(u768, inv, tc, r768, A.mult, A.mult).then_inc(e7, 1)
+    v.tensor_scalar(cn, inv, -1.0 / NT, None, A.mult).then_inc(e8, 1)
 
     w = N * NS
     MS, S1, SD, CK, KK = (T.land[:, i:w:NS] for i in (0, 1, 3, 4, 7))
     S2E = T.land[:, 2:w:4]
-    c1, c2, c3, c4, c8, c9, c10, c14, c15, c16 = (new() for _ in range(10))
-    f1, f2, f3, f4, f5, f6, f7 = (new() for _ in range(7))
+    c1, c2, c3, c4, c8, c9, c10, c11, c12, c14, c16 = (new() for _ in range(11))
+    f1, f3, f4, f5, f6, f7, f8 = (new() for _ in range(7))
     d1, d2, d3 = (new() for _ in range(3))
-    smn, ss2, nssd, bcol, na, gown, vv, rp, s768, nb, db, acc, sd = (column() for _ in range(13))
-    kq = float(TK) / float(NT * NT)
-    r768 = math.sqrt(float(NT))
+    smn, ss2, bcol, na, gown, vv, rp, s768, nb, db, acc, sd, rsn = (column() for _ in range(13))
 
     s.wait_ge(sem.near, near)
     s.wait_ge(sem.far, far)
-    s.wait_ge(a2, 1)
     s.wait_ge(sem.vs, nvs)
+    s.wait_ge(sem.ss, nss)
     s.activation(T.j6a[:, 0:N], S1, F.Square, scale=math.sqrt(1.0 / TK), accum_out=db).then_inc(d1, 1)
+    s.activation(T.j6c[:, 0:N], SD, F.Copy, scale=-1.0 / NT, accum_out=na).then_inc(f5, 1)
     s.wait_ge(c1, 1)
     s.activation(T.j6b[:, 0:N], MS, F.Square, bias=smn, scale=float(N), accum_out=acc).then_inc(d2, 1)
     s.wait_ge(d2, 1)
     s.wait_ge(f4, 1)
-    s.activation(sd, acc, F.Sqrt, bias=bcol, scale=kq).then_inc(d3, 1)
+    s.wait_ge(e6, 1)
+    s.activation(sd, acc, F.Sqrt, bias=bcol, scale=kqi).then_inc(d3, 1)
+    s.wait_ge(f5, 1)
+    s.activation(T.ya[:], T.dys[:], F.Identity, bias=na).then_inc(f7, 1)
+    s.wait_ge(f7, 1)
+    s.wait_ge(c11, 1)
+    s.activation(T.yb[:], T.ya[:], F.Identity, scale=rsn).then_inc(f8, 1)
 
     ndk = T.ndk[:, 0:N]
     v.wait_ge(sem.near, near)
     v.wait_ge(sem.far, far)
     v.wait_ge(b1, 1)
-    v.wait_ge(b2, 1)
-    v.wait_ge(sem.vs, nvs)
     v.tensor_reduce(smn, MS, X, A.add, negate=True).then_inc(c1, 1)
     v.tensor_reduce(ss2, S2E, X, A.add).then_inc(f1, 1)
-    v.tensor_reduce(nssd, SD, X, A.add, negate=True).then_inc(f2, 1)
-    v.tensor_scalar(T.t12[:, N:2 * N], CK, float(NT), None, A.mult).then_inc(f3, 1)
     v.wait_ge(d1, 1)
     v.wait_ge(f1, 1)
-    v.tensor_scalar(bcol, db, -1.0, ss2, A.mult, A.add).then_inc(f4, 1)
+    v.tensor_scalar(bcol, ss2, db, inv, A.subtract, A.mult).then_inc(f4, 1)
     v.wait_ge(c1, 1)
     v.tensor_scalar(ndk, KK, float(NT), smn, A.mult, A.add).then_inc(c2, 1)
-    v.wait_ge(f2, 1)
-    v.tensor_scalar(na, nssd, 1.0 / NT, None, A.mult).then_inc(f5, 1)
+    v.tensor_scalar(T.t12[:, N:2 * N], CK, float(NT), None, A.mult).then_inc(f3, 1)
     v.wait_ge(c2, 1)
     v.tensor_tensor(T.t12[:, 0:N], ndk, SD, A.mult).then_inc(c3, 1)
     v.tensor_scalar(gown, T.ndk[:, slot[core]:slot[core] + 1], 1.0 / NT, None, A.mult).then_inc(f6, 1)
     v.wait_ge(d2, 1)
     v.wait_ge(f4, 1)
-    v.tensor_scalar(vv, acc, kq, bcol, A.mult, A.add).then_inc(c8, 1)
-    v.wait_ge(f5, 1)
-    v.tensor_scalar(T.ya[:], T.dys[:], na, r768, A.add, A.mult).then_inc(f7, 1)
+    v.wait_ge(e6, 1)
+    v.tensor_scalar(vv, acc, kqi, bcol, A.mult, A.add).then_inc(c8, 1)
     v.wait_ge(c3, 1)
     v.wait_ge(f3, 1)
     v.tensor_reduce(s768, T.t12[:], X, A.add).then_inc(c4, 1)
     v.wait_ge(c8, 1)
     v.reciprocal(rp, vv).then_inc(c9, 1)
+    v.wait_ge(f6, 1)
+    v.tensor_scalar(xg, xc, gown, None, A.add).then_inc(c12, 1)
     v.wait_ge(c4, 1)
     v.wait_ge(c9, 1)
-    v.tensor_scalar(nb, s768, rp, -1.0 / r768, A.mult, A.mult).then_inc(c10, 1)
-    v.wait_ge(c10, 1)
-    v.wait_ge(f6, 1)
-    v.tensor_scalar(t2, xc, gown, nb, A.add, A.mult).then_inc(c14, 1)
-    v.wait_ge(c14, 1)
-    v.wait_ge(f7, 1)
-    v.tensor_tensor(T.br[:], T.ya[:], t2, A.add).then_inc(c15, 1)
-    v.wait_ge(c15, 1)
+    v.wait_ge(e8, 1)
+    v.tensor_scalar(nb, s768, rp, cn, A.mult, A.mult).then_inc(c10, 1)
     v.wait_ge(d3, 1)
-    v.tensor_scalar(T.out[:], T.br[:], rp, sd, A.mult, A.mult).then_inc(c16, 1)
+    v.wait_ge(e7, 1)
+    v.tensor_scalar(rsn, rp, sd, u768, A.mult, A.mult).then_inc(c11, 1)
+    v.wait_ge(c10, 1)
+    v.wait_ge(c11, 1)
+    v.wait_ge(c12, 1)
+    v.tensor_scalar(t2, xg, nb, rsn, A.mult, A.mult).then_inc(c14, 1)
+    v.wait_ge(c14, 1)
+    v.wait_ge(f8, 1)
+    v.tensor_tensor(T.out[:], T.yb[:], t2, A.add).then_inc(c16, 1)
 
     sy.wait_ge(c16, 1)
     sy.dma_start(T.dx[:], T.out[:]).then_inc(sem.st, 16)

import math
from concourse.bass import DstId, RemoteDMATransfer
from concourse.mybir import AluOpType, AxisListType, ActivationFunctionType

N = 6
TK = 128
NT = N * TK
EPS = 0.01
NS = 8
ENGINES = 8

SCRATCH = {
    "xs": ("sbuf", [128, TK], "float32"),
    "dys": ("sbuf", [128, TK], "float32"),
    "land": ("sbuf", [128, N * NS], "float32"),
    "col": ("sbuf", [128, 32], "float32"),
    "j2": ("sbuf", [128, TK], "float32"),
    "j3": ("sbuf", [128, TK], "float32"),
    "j4": ("sbuf", [128, TK], "float32"),
    "prod": ("sbuf", [128, TK], "float32"),
    "j6a": ("sbuf", [128, 8], "float32"),
    "j6b": ("sbuf", [128, 8], "float32"),
    "j6c": ("sbuf", [128, 8], "float32"),
    "ndk": ("sbuf", [128, 8], "float32"),
    "t12": ("sbuf", [128, 2 * N], "float32"),
    "ya": ("sbuf", [128, TK], "float32"),
    "yb": ("sbuf", [128, TK], "float32"),
    "out": ("sbuf", [128, TK], "float32"),
    "xc": ("psum", [128, 512], "float32"),
    "xg": ("psum", [128, 512], "float32"),
    "t2": ("psum", [128, 512], "float32"),
}
SEMAPHORES = ["ldx", "ldy", "st", "near", "far", "sent", "vs", "ss"] + ["k%d" % i for i in range(48)]


def _low(mask, n):
    out, b = 0, 1
    while n > 0:
        if mask & b:
            out |= b
            n -= 1
        b <<= 1
    return out


def _count(mask):
    return bin(mask).count("1")


def _plan(T, topo):
    cores = list(T.cores)
    chips = []
    for c in cores:
        if topo.chip(c) not in chips:
            chips.append(topo.chip(c))
    order = [c for ch in chips for c in cores if topo.chip(c) == ch]
    slot = {c: i for i, c in enumerate(order)}
    home = {c: [d for d in order if topo.chip(d) == topo.chip(c)] for c in cores}
    away = {c: [d for d in order if topo.chip(d) != topo.chip(c)] for c in cores}
    far = {c: [] for c in cores}
    for ch in chips:
        ranks = [c for c in order if topo.chip(c) == ch]
        can = {d: [c for c in ranks if topo.may_write(c, d)] for d in away[ranks[0]]}
        for d in sorted(can, key=lambda e: len(can[e])):
            c = min(can[d], key=lambda e: (len(far[e]), topo.die(e) != topo.die(d)))
            far[c].append(d)
    mask = {}
    for c in cores:
        m = -1
        for d in [e for e in home[c] if e != c] + far[c]:
            m &= topo.mask(c, d)
        mask[c] = _low(m, min(ENGINES, _count(m)))
    return slot, home, far, mask


def rank_program(g, core, T, topo):
    if T.rank_of(core) is None:
        return
    slot, home, far_of, mask = _plan(T, topo)
    v, s, sy = g.vector, g.scalar, g.sync
    sem = T.sem
    A, X, F = AluOpType, AxisListType.X, ActivationFunctionType
    nk = [0]

    def new():
        nk[0] += 1
        return sem["k%d" % (nk[0] - 1)]

    ncol = [0]

    def column():
        ncol[0] += 1
        return T.col[:, ncol[0] - 1:ncol[0]]

    def write(dests, src, dst, remote_sem):
        g.remote_dma_fused(
            [RemoteDMATransfer(dst_ids=[DstId(rid=topo.addr(d)[0], pnc=topo.addr(d)[1]) for d in dests],
                               dma_engine_mask=mask[core], remote_sem=remote_sem,
                               srcs=[src], dsts=[dst for _ in dests], alu_op=0)],
            local_sem=sem.sent)
        return _count(mask[core])

    o = slot[core] * NS
    o_m, o_s1, o_s2, o_sd, o_ck, o_p0, o_pe, o_k = (T.land[:, o + i:o + i + 1] for i in range(NS))
    xc = T.xc[:, 0:TK]
    xg = T.xg[:, 0:TK]
    t2 = T.t2[:, 0:TK]
    first = T.xs[:, 0:1]
    mates = [d for d in home[core] if d != core]

    sy.dma_start(T.xs[:], T.x[:]).then_inc(sem.ldx, 16)
    s.dma_start(T.dys[:], T.dy[:]).then_inc(sem.ldy, 16)

    g.wait_ge(sem.ldx, 16)
    sent = write(mates, first, o_k, sem.near)

    a1, a3, b1 = (new() for _ in range(3))
    v.memset(o_p0, 0.0).then_inc(sem.vs, 1)
    v.memset(o_pe, TK * EPS).then_inc(sem.vs, 1)
    v.wait_ge(sem.ldx, 16)
    v.tensor_scalar(xc, T.xs[:], first, None, A.subtract).then_inc(a1, 1)
    v.wait_ge(sem.ldy, 16)
    v.wait_ge(a1, 1)
    v.tensor_tensor(T.prod[:], T.dys[:], xc, A.mult).then_inc(a3, 1)
    v.tensor_reduce(o_s1, xc, X, A.add).then_inc(sem.vs, 1)
    v.wait_ge(a3, 1)
    v.tensor_reduce(o_ck, T.prod[:], X, A.add).then_inc(sem.vs, 1)
    nvs = 4

    s.wait_ge(sem.ldx, 16)
    s.activation(T.j2[:], T.xs[:], F.Square, bias=first, scale=-1.0, accum_out=o_s2).then_inc(sem.ss, 1)
    s.activation(T.j3[:], T.xs[:], F.Copy, accum_out=o_m).then_inc(sem.ss, 1)
    s.wait_ge(sem.ldy, 16)
    s.activation(T.j4[:], T.dys[:], F.Copy, accum_out=o_sd).then_inc(sem.ss, 1)
    s.activation(o_k, first, F.Copy).then_inc(b1, 1)
    nss = 3

    g.wait_ge(sem.ss, nss)
    g.wait_ge(sem.vs, nvs)
    rest = T.land[:, o:o + NS - 1]
    sent += write(mates, rest, rest, sem.near)
    near = sum(2 * _count(mask[d]) for d in mates)
    if far_of[core]:
        lo = min(slot[d] for d in home[core]) * NS
        block = T.land[:, lo:lo + NS * len(home[core])]
        g.wait_ge(b1, 1)
        g.wait_ge(sem.near, near)
        sent += write(far_of[core], block, block, sem.far)
    g.wait_ge(sem.sent, sent)
    far = sum(_count(mask[c]) for c in far_of if core in far_of[c])

    kq = float(TK) / float(NT * NT)
    r768 = math.sqrt(float(NT))

    e1, e2, e3, e4, e5, e6, e7, e8 = (new() for _ in range(8))
    q1, own, tc, tt, inv, kqi, u768, cn = (column() for _ in range(8))
    v.wait_ge(sem.vs, nvs)
    v.wait_ge(sem.ss, nss)
    v.tensor_scalar(q1, o_s1, o_s1, -1.0 / TK, A.mult, A.mult).then_inc(e1, 1)
    v.wait_ge(e1, 1)
    v.tensor_scalar(own, q1, o_s2, TK * EPS, A.add, A.add).then_inc(e2, 1)
    s.wait_ge(e2, 1)
    s.activation(tc, own, F.Sqrt).then_inc(e3, 1)
    v.wait_ge(e3, 1)
    v.tensor_scalar(tt, tc, tc, None, A.mult).then_inc(e4, 1)
    v.wait_ge(e4, 1)
    v.reciprocal(inv, tt).then_inc(e5, 1)
    v.wait_ge(e5, 1)
    v.tensor_scalar(kqi, inv, kq, None, A.mult).then_inc(e6, 1)
    v.tensor_scalar(u768, inv, tc, r768, A.mult, A.mult).then_inc(e7, 1)
    v.tensor_scalar(cn, inv, -1.0 / NT, None, A.mult).then_inc(e8, 1)

    w = N * NS
    MS, S1, SD, CK, KK = (T.land[:, i:w:NS] for i in (0, 1, 3, 4, 7))
    S2E = T.land[:, 2:w:4]
    c1, c2, c3, c4, c8, c9, c10, c11, c12, c14, c16 = (new() for _ in range(11))
    f1, f3, f4, f5, f6, f7, f8 = (new() for _ in range(7))
    d1, d2, d3 = (new() for _ in range(3))
    smn, ss2, bcol, na, gown, vv, rp, s768, nb, db, acc, sd, rsn = (column() for _ in range(13))

    s.wait_ge(sem.near, near)
    s.wait_ge(sem.far, far)
    s.wait_ge(sem.vs, nvs)
    s.wait_ge(sem.ss, nss)
    s.activation(T.j6a[:, 0:N], S1, F.Square, scale=math.sqrt(1.0 / TK), accum_out=db).then_inc(d1, 1)
    s.activation(T.j6c[:, 0:N], SD, F.Copy, scale=-1.0 / NT, accum_out=na).then_inc(f5, 1)
    s.wait_ge(c1, 1)
    s.activation(T.j6b[:, 0:N], MS, F.Square, bias=smn, scale=float(N), accum_out=acc).then_inc(d2, 1)
    s.wait_ge(d2, 1)
    s.wait_ge(f4, 1)
    s.wait_ge(e6, 1)
    s.activation(sd, acc, F.Sqrt, bias=bcol, scale=kqi).then_inc(d3, 1)
    s.wait_ge(f5, 1)
    s.activation(T.ya[:], T.dys[:], F.Identity, bias=na).then_inc(f7, 1)
    s.wait_ge(f7, 1)
    s.wait_ge(c11, 1)
    s.activation(T.yb[:], T.ya[:], F.Identity, scale=rsn).then_inc(f8, 1)

    ndk = T.ndk[:, 0:N]
    v.wait_ge(sem.near, near)
    v.wait_ge(sem.far, far)
    v.wait_ge(b1, 1)
    v.tensor_reduce(smn, MS, X, A.add, negate=True).then_inc(c1, 1)
    v.tensor_reduce(ss2, S2E, X, A.add).then_inc(f1, 1)
    v.wait_ge(d1, 1)
    v.wait_ge(f1, 1)
    v.tensor_scalar(bcol, ss2, db, inv, A.subtract, A.mult).then_inc(f4, 1)
    v.wait_ge(c1, 1)
    v.tensor_scalar(ndk, KK, float(NT), smn, A.mult, A.add).then_inc(c2, 1)
    v.tensor_scalar(T.t12[:, N:2 * N], CK, float(NT), None, A.mult).then_inc(f3, 1)
    v.wait_ge(c2, 1)
    v.tensor_tensor(T.t12[:, 0:N], ndk, SD, A.mult).then_inc(c3, 1)
    v.tensor_scalar(gown, T.ndk[:, slot[core]:slot[core] + 1], 1.0 / NT, None, A.mult).then_inc(f6, 1)
    v.wait_ge(d2, 1)
    v.wait_ge(f4, 1)
    v.wait_ge(e6, 1)
    v.tensor_scalar(vv, acc, kqi, bcol, A.mult, A.add).then_inc(c8, 1)
    v.wait_ge(c3, 1)
    v.wait_ge(f3, 1)
    v.tensor_reduce(s768, T.t12[:], X, A.add).then_inc(c4, 1)
    v.wait_ge(c8, 1)
    v.reciprocal(rp, vv).then_inc(c9, 1)
    v.wait_ge(f6, 1)
    v.tensor_scalar(xg, xc, gown, None, A.add).then_inc(c12, 1)
    v.wait_ge(c4, 1)
    v.wait_ge(c9, 1)
    v.wait_ge(e8, 1)
    v.tensor_scalar(nb, s768, rp, cn, A.mult, A.mult).then_inc(c10, 1)
    v.wait_ge(d3, 1)
    v.wait_ge(e7, 1)
    v.tensor_scalar(rsn, rp, sd, u768, A.mult, A.mult).then_inc(c11, 1)
    v.wait_ge(c10, 1)
    v.wait_ge(c11, 1)
    v.wait_ge(c12, 1)
    v.tensor_scalar(t2, xg, nb, rsn, A.mult, A.mult).then_inc(c14, 1)
    v.wait_ge(c14, 1)
    v.wait_ge(f8, 1)
    v.tensor_tensor(T.out[:], T.yb[:], t2, A.add).then_inc(c16, 1)

    sy.wait_ge(c16, 1)
    sy.dma_start(T.dx[:], T.out[:]).then_inc(sem.st, 16)
    sy.wait_ge(sem.st, 16)
